import numpy as np
import ml_dtypes


def mxq(x, axis, fmt="e4m3"):
    dtype, down = {"e4m3": (ml_dtypes.float8_e4m3fn, 7), "e5m2": (ml_dtypes.float8_e5m2, 14)}[fmt]
    v = np.moveaxis(np.asarray(x, np.float32).astype(ml_dtypes.bfloat16).astype(np.float64), axis, -1)
    blocks = v.reshape(v.shape[:-1] + (-1, 32))
    amax = np.abs(blocks).max(-1, keepdims=True)
    byte = np.maximum(np.where(amax > 0, np.frexp(amax)[1] - 1 + 127, 0) - down, 1)
    scale = np.exp2(byte - 127.0)
    codes = (blocks / scale).astype(np.float32).astype(dtype).astype(np.float64)
    return np.moveaxis((codes * scale).reshape(v.shape), -1, axis)


WIDE = False


def mx_kscale(k):
    if not WIDE:
        return np.ones(k)
    levels = np.array([10, -10, 5, -5, 0])
    if k % 512:
        return np.exp2(np.random.permutation(np.resize(levels, k // 32))).repeat(32)
    a = np.empty((k // 512, 16))
    for p in range(k // 512):
        a[p, :8] = np.random.permutation(np.resize(levels, 8))
        for g in range(8):
            far = levels[np.abs(levels - a[p, g]) >= 10]
            a[p, g + 8] = far[np.random.randint(len(far))]
    return np.exp2(a.ravel()).repeat(32)


def f64(x):
    return np.asarray(x).astype(np.float64)


def striped(idx):
    return np.tile(idx.reshape(-1, 16).T, (8, 1)).astype(np.uint16)


def unstriped(offs):
    return offs[:16].T.reshape(-1).astype(np.int64)


E2M1 = np.array([0.0, 0.5, 1.0, 1.5, 2.0, 3.0, 4.0, 6.0, -0.0, -0.5, -1.0, -1.5, -2.0, -3.0, -4.0, -6.0])


def pack_weight(w, fmt):
    k, n = w.shape
    w = f64(np.asarray(w, np.float32).astype(ml_dtypes.bfloat16)).reshape(k // 32, 32, n)
    amax = np.abs(w).max(1)
    if fmt == "e4m3":
        byte = np.frexp(amax)[1] - 1 + 127 - 7
    else:
        mant, ex = np.frexp(amax / 6.0)
        byte = np.where(mant > 0.5, ex, ex - 1) + 127
    byte = np.clip(np.where(amax > 0, byte, 1), 1, 254)
    scaled = (w * np.exp2(127.0 - byte)[:, None, :]).reshape(k, n).astype(np.float32)
    by_word = np.ascontiguousarray(scaled.reshape(k // 512, 128, 4, n).transpose(0, 1, 3, 2))
    if fmt == "e4m3":
        words = by_word.astype(ml_dtypes.float8_e4m3fn).view(np.uint8)
    else:
        c = by_word.astype(ml_dtypes.float4_e2m1fn).view(np.uint8) & 0xF
        words = (c[..., 0::2] | (c[..., 1::2] << 4)).reshape(k // 512, 128, 2 * n)
    return np.ascontiguousarray(words), np.ascontiguousarray(byte.astype(np.uint8).reshape(k // 512, 16, n))


def unpack_weight(words, scales, fmt):
    g, _, n = scales.shape
    words = np.ascontiguousarray(words).reshape(g, 128, n, -1)
    if fmt == "e4m3":
        vals = words.view(ml_dtypes.float8_e4m3fn).astype(np.float64)
    else:
        nib = np.empty((g, 128, n, 4), np.uint8)
        nib[..., 0::2] = words & 0xF
        nib[..., 1::2] = words >> 4
        vals = E2M1[nib]
    vals = vals * np.repeat(np.exp2(scales.astype(np.float64) - 127.0), 8, axis=1)[..., None]
    return vals.transpose(0, 1, 3, 2).reshape(g * 512, n)


def relu2(v):
    return np.maximum(v, 0.0) ** 2


K, T, E, C, N = 1024, 1024, 8, 128, 512
K8 = 512


def by_expert(wq, xq):
    return np.concatenate([wq[e].T @ xq[:, e * C:(e + 1) * C] for e in range(E)], axis=1)


def setup_inputs():
    n = np.random.standard_normal
    s = mx_kscale(K)[:, None]
    w = n((E, K, N)) / np.sqrt(K) / s[None]
    w8 = [pack_weight(m[:K8], "e4m3") for m in w]
    w4 = [pack_weight(m[K8:], "e2m1") for m in w]
    return {
        "xT": (n((K, T)) * s).astype(np.float32),
        "w8_words": np.stack([m[0] for m in w8]),
        "w8_scales": np.stack([m[1] for m in w8]),
        "w4_words": np.stack([m[0] for m in w4]),
        "w4_scales": np.stack([m[1] for m in w4]),
        "b": (0.3 * n((N, E))).astype(np.float32),
        "gate": np.tile(np.random.uniform(0.2, 1.0, E * C), (N, 1)).astype(np.float32),
        "offs": striped(np.random.permutation(T)[:E * C]),
        "dst": striped(np.random.permutation(T)[:E * C]),
    }


def reference(xT, w8_words, w8_scales, w4_words, w4_scales, b, gate, offs, dst):
    idx = unstriped(offs)
    w = np.stack([np.concatenate([unpack_weight(w8_words[e], w8_scales[e], "e4m3"), unpack_weight(w4_words[e], w4_scales[e], "e2m1")]) for e in range(E)])
    xq = mxq(f64(xT)[:, idx], 0, "e4m3")
    y = by_expert(w, xq)
    y = relu2(y + np.repeat(f64(b), C, axis=1))
    out = np.zeros((N, T))
    out[:, unstriped(dst)] = f64(gate) * y
    return out

@@ -1,0 +1,157 @@
+import concourse.mybir as mybir
+
+K, T, E, C, N = 1024, 1024, 8, 128, 512
+P = 128
+J = 4
+FLOPS = 2 * K * N * E * C
+BYTES = K * T * 4 + E * 128 * 512 * 6 + 2 * E * 16 * 512 + N * E * 4 + T * 4 + 2 * P * 64 * 2 + N * T * 4
+
+F32 = mybir.dt.float32
+BF16 = mybir.dt.bfloat16
+U32 = mybir.dt.uint32
+I32 = mybir.dt.int32
+U16 = mybir.dt.uint16
+U8 = mybir.dt.uint8
+FP8X4 = mybir.dt.float8_e4m3fn_x4
+FP4X4 = mybir.dt.float4_e2m1fn_x4
+RELU = mybir.ActivationFunctionType.Relu
+SQUARE = mybir.ActivationFunctionType.Square
+MULT = mybir.AluOpType.mult
+
+NT = N // P
+HALF = T // 2
+CHUNKS = (
+    ((0, 512, 320), (512, 256, 160), (768, 256, 160)),
+    ((0, 512, 192), (512, 256, 128), (768, 256, 160)),
+)
+PLANE = (4, 0)
+
+
+def tile_moe_two_lin_relu2_kernel(tc, xT, w8_words, w8_scales, w4_words, w4_scales, b, gate, offs, dst, out):
+    nc = tc.nc
+    with tc.tile_pool(name="keep", bufs=1) as keep, tc.psum_pool(name="psum", bufs=1) as psum:
+        offs_t = keep.tile([P, 64], U16, name="offs_t")
+        dst_t = keep.tile([P, 64], U16, name="dst_t")
+        bias = keep.tile([P, NT, E], F32, name="bias")
+        gate_t = keep.tile([P, T], F32, name="gate_t")
+        words = [keep.tile([P, T], U32, name=f"words{a}", align_bytes=256) for a in range(2)]
+        scales = keep.tile([P, T], U8, name="scales", align_bytes=256)
+        g_words = [keep.tile([P, T], U32, name=f"g_words{a}", align_bytes=256) for a in range(2)]
+        g_scales = keep.tile([P, T], U8, name="g_scales", align_bytes=256)
+        w8_t = keep.tile([P, E, 4 * N], U8, name="w8_t", align_bytes=256)
+        w4_t = keep.tile([P, E, 2 * N], U8, name="w4_t", align_bytes=256)
+        w_sc = keep.tile([P, E * N], U8, name="w_sc", align_bytes=256)
+        window = [keep.tile([P, T], F32, name=f"window{n}") for n in range(NT)]
+        banks = [[psum.tile([P, HALF], F32, name=f"bank{n}_{h}") for h in range(2)] for n in range(NT)]
+
+        nc.gpsimd.memset(scales[:], 0)
+        nc.vector.memset(w_sc[:].bitcast(I32), 0)
+
+        x_view = xT.rearrange("(a p j) t -> a p j t", a=2, j=J)
+        raws, grouped = {}, {}
+        for a in range(2):
+            for i, (t0, width, v) in enumerate(CHUNKS[a]):
+                raws[a, i] = keep.tile([P, J, width], F32, name=f"raw{a}_{i}")
+                grouped[a, i] = keep.tile([P, width, J], BF16, name=f"grouped{a}_{i}", align_bytes=256)
+                nc.sync.dma_start(out=raws[a, i][:], in_=x_view[a][:, :, t0 : t0 + width])
+                if (a, i) == (0, 0):
+                    nc.sync.dma_start(offs_t[:], offs)
+                if (a, i) == (0, 1):
+                    nc.sync.dma_start(dst_t[:], dst)
+                if (a, i) == (0, 2):
+                    nc.sync.dma_start(out=bias[:], in_=b.rearrange("(n p) e -> p n e", p=P))
+
+        def load_weights(e0, e1):
+            nc.sync.dma_start(
+                out=w8_t[:, e0:e1, :].bitcast(I32),
+                in_=w8_words[e0:e1].rearrange("e a p n r -> (a p) e (n r)").bitcast(I32),
+            )
+            nc.sync.dma_start(
+                out=w4_t[:, e0:e1, :].bitcast(I32), in_=w4_words[e0:e1].rearrange("e a p n -> (a p) e n").bitcast(I32)
+            )
+
+        def load_gate(h):
+            nc.sync.dma_start(out=gate_t[:, h * HALF : (h + 1) * HALF], in_=gate[0:P, h * HALF : (h + 1) * HALF])
+
+        load_weights(0, 2)
+        for r in range(4):
+            for plane, sc in ((0, w4_scales), (4, w8_scales)):
+                nc.sync.dma_start(
+                    out=w_sc[plane + r : P : 32, :].bitcast(I32).rearrange("q (e n) -> q e n", e=E),
+                    in_=sc.bitcast(I32).rearrange("e a (q r) n -> r a q e n", r=4)[r][0],
+                )
+        load_weights(2, 4)
+        load_gate(0)
+        load_weights(4, 6)
+        load_weights(6, 8)
+        load_gate(1)
+
+        def interleave(a, i):
+            t0, width, v = CHUNKS[a][i]
+            for copy, lo, hi in ((nc.vector.tensor_copy, 0, v), (nc.scalar.copy, v, width)):
+                copy(
+                    out=grouped[a, i][:, lo:hi, :].rearrange("p (c i) j -> p c j i", i=4),
+                    in_=raws[a, i][:, :, lo:hi].rearrange("p j (c i) -> p c j i", i=4),
+                )
+
+        def quantise(a, i):
+            t0, width, v = CHUNKS[a][i]
+            nc.vector.quantize_mx(
+                out=words[a][:, t0 : t0 + width].bitcast(FP8X4),
+                scales=scales[PLANE[a] : P, t0 : t0 + width],
+                in_=grouped[a, i][:].rearrange("p t j -> p (t j)"),
+            )
+
+        def gather(to, of, h):
+            nc.vector.tensor_copy(to[:, h * HALF : (h + 1) * HALF], of[:].indirect(offs_t[:, 32 * h : 32 * h + 32]))
+
+        for a in range(2):
+            interleave(a, 0)
+            interleave(a, 1)
+            quantise(a, 0)
+            interleave(a, 2)
+            quantise(a, 1)
+            quantise(a, 2)
+            if a == 0:
+                gather(g_words[0], words[0], 0)
+                gather(g_words[0], words[0], 1)
+        for h in range(2):
+            gather(g_scales, scales, h)
+            gather(g_words[1], words[1], h)
+
+        for n, h in ((0, 0), (1, 0), (0, 1), (1, 1), (2, 0), (3, 0), (2, 1), (3, 1)):
+            relu = keep.tile([P, HALF], F32, name=f"relu{n}_{h}")
+            squared = keep.tile([P, HALF], F32, name=f"squared{n}_{h}")
+            for q in range(4):
+                e = 4 * h + q
+                place = slice(q * C, (q + 1) * C)
+                slots = slice(e * C, (e + 1) * C)
+                w_cols = slice(e * N + n * P, e * N + (n + 1) * P)
+                nc.tensor.matmul_mx(
+                    out=banks[n][h][:, place],
+                    lhsT=w8_t[:, e, 4 * n * P : 4 * (n + 1) * P].bitcast(FP8X4),
+                    lhsT_scale=w_sc[4:P, w_cols],
+                    rhs=g_words[0][:, slots].bitcast(FP8X4),
+                    rhs_scale=g_scales[4:P, slots],
+                    start=True,
+                    stop=False,
+                )
+                nc.tensor.matmul_mx(
+                    out=banks[n][h][:, place],
+                    lhsT=w4_t[:, e, 2 * n * P : 2 * (n + 1) * P].bitcast(FP4X4),
+                    lhsT_scale=w_sc[:, w_cols],
+                    rhs=g_words[1][:, slots].bitcast(FP8X4),
+                    rhs_scale=g_scales[:, slots],
+                    start=False,
+                    stop=True,
+                )
+                nc.scalar.activation(relu[:, place], banks[n][h][:, place], RELU, bias=bias[:, n, e : e + 1])
+            nc.scalar.activation(squared[:], relu[:], SQUARE)
+            nc.vector.tensor_tensor(
+                window[n][:].indirect(dst_t[:, 32 * h : 32 * h + 32]),
+                squared[:],
+                gate_t[:, h * HALF : (h + 1) * HALF],
+                MULT,
+            )
+            if h == 1:
+                nc.sync.dma_start(out=out[n * P : (n + 1) * P, :], in_=window[n][:])

@@ -21,10 +21,14 @@ MULT = mybir.AluOpType.mult
 NT = N // P
 HALF = T // 2
 CHUNKS = (
-    ((0, 512, 320), (512, 256, 160), (768, 256, 160)),
-    ((0, 512, 192), (512, 256, 128), (768, 256, 160)),
+    ((0, 512, 320), (512, 512, 320)),
+    ((0, 512, 160), (512, 256, 128), (768, 256, 160)),
 )
 PLANE = (4, 0)
+PIECES = (
+    (0, 0, 2), (1, 0, 2), (0, 2, 4), (1, 2, 4), (0, 4, 8), (1, 4, 8),
+    (2, 0, 4), (3, 0, 4), (2, 4, 8), (3, 4, 8),
+)
 
 
 def tile_moe_two_lin_relu2_kernel(tc, xT, w8_words, w8_scales, w4_words, w4_scales, b, gate, offs, dst, out):
@@ -47,43 +51,51 @@ def tile_moe_two_lin_relu2_kernel(tc, xT, w8_words, w8_scales, w4_words, w4_scal
         nc.gpsimd.memset(scales[:], 0)
         nc.vector.memset(w_sc[:].bitcast(I32), 0)
 
+        def load_w8(e0, e1):
+            nc.sync.dma_start(
+                out=w8_t[:, e0:e1, :].bitcast(I32),
+                in_=w8_words[e0:e1].rearrange("e a p n r -> (a p) e (n r)").bitcast(I32),
+            )
+
+        def load_w4(e0, e1):
+            nc.sync.dma_start(
+                out=w4_t[:, e0:e1, :].bitcast(I32), in_=w4_words[e0:e1].rearrange("e a p n -> (a p) e n").bitcast(I32)
+            )
+
+        def load_scales(r):
+            for plane, sc in ((0, w4_scales), (4, w8_scales)):
+                nc.sync.dma_start(
+                    out=w_sc[plane + r : P : 32, :].bitcast(I32).rearrange("q (e n) -> q e n", e=E),
+                    in_=sc.bitcast(I32).rearrange("e a (q r) n -> r a q e n", r=4)[r][0],
+                )
+
+        def load_gate(h):
+            nc.sync.dma_start(out=gate_t[:, h * HALF : (h + 1) * HALF], in_=gate[0:P, h * HALF : (h + 1) * HALF])
+
         x_view = xT.rearrange("(a p j) t -> a p j t", a=2, j=J)
         raws, grouped = {}, {}
         for a in range(2):
             for i, (t0, width, v) in enumerate(CHUNKS[a]):
                 raws[a, i] = keep.tile([P, J, width], F32, name=f"raw{a}_{i}")
                 grouped[a, i] = keep.tile([P, width, J], BF16, name=f"grouped{a}_{i}", align_bytes=256)
+                if (a, i) == (1, 2):
+                    load_scales(0)
+                    load_scales(1)
                 nc.sync.dma_start(out=raws[a, i][:], in_=x_view[a][:, :, t0 : t0 + width])
                 if (a, i) == (0, 0):
                     nc.sync.dma_start(offs_t[:], offs)
-                if (a, i) == (0, 1):
-                    nc.sync.dma_start(dst_t[:], dst)
-                if (a, i) == (0, 2):
-                    nc.sync.dma_start(out=bias[:], in_=b.rearrange("(n p) e -> p n e", p=P))
 
-        def load_weights(e0, e1):
-            nc.sync.dma_start(
-                out=w8_t[:, e0:e1, :].bitcast(I32),
-                in_=w8_words[e0:e1].rearrange("e a p n r -> (a p) e (n r)").bitcast(I32),
-            )
-            nc.sync.dma_start(
-                out=w4_t[:, e0:e1, :].bitcast(I32), in_=w4_words[e0:e1].rearrange("e a p n -> (a p) e n").bitcast(I32)
-            )
-
-        def load_gate(h):
-            nc.sync.dma_start(out=gate_t[:, h * HALF : (h + 1) * HALF], in_=gate[0:P, h * HALF : (h + 1) * HALF])
-
-        load_weights(0, 2)
-        for r in range(4):
-            for plane, sc in ((0, w4_scales), (4, w8_scales)):
-                nc.sync.dma_start(
-                    out=w_sc[plane + r : P : 32, :].bitcast(I32).rearrange("q (e n) -> q e n", e=E),
-                    in_=sc.bitcast(I32).rearrange("e a (q r) n -> r a q e n", r=4)[r][0],
-                )
-        load_weights(2, 4)
+        load_w8(0, 2)
+        load_scales(2)
+        load_scales(3)
+        nc.sync.dma_start(out=bias[:], in_=b.rearrange("(n p) e -> p n e", p=P))
+        load_w4(0, 4)
+        load_w8(2, 4)
         load_gate(0)
-        load_weights(4, 6)
-        load_weights(6, 8)
+        nc.sync.dma_start(dst_t[:], dst)
+        load_w8(4, 6)
+        load_w4(4, 8)
+        load_w8(6, 8)
         load_gate(1)
 
         def interleave(a, i):
@@ -102,33 +114,37 @@ def tile_moe_two_lin_relu2_kernel(tc, xT, w8_words, w8_scales, w4_words, w4_scal
                 in_=grouped[a, i][:].rearrange("p t j -> p (t j)"),
             )
 
-        def gather(to, of, h):
-            nc.vector.tensor_copy(to[:, h * HALF : (h + 1) * HALF], of[:].indirect(offs_t[:, 32 * h : 32 * h + 32]))
+        def gather(to, of, e0, e1):
+            nc.vector.tensor_copy(to[:, e0 * C : e1 * C], of[:].indirect(offs_t[:, 8 * e0 : 8 * e1]))
 
-        for a in range(2):
-            interleave(a, 0)
-            interleave(a, 1)
-            quantise(a, 0)
-            interleave(a, 2)
-            quantise(a, 1)
-            quantise(a, 2)
-            if a == 0:
-                gather(g_words[0], words[0], 0)
-                gather(g_words[0], words[0], 1)
-        for h in range(2):
-            gather(g_scales, scales, h)
-            gather(g_words[1], words[1], h)
+        interleave(0, 0)
+        interleave(0, 1)
+        quantise(0, 0)
+        quantise(0, 1)
+        gather(g_words[0], words[0], 0, 4)
+        gather(g_words[0], words[0], 4, 8)
+        interleave(1, 0)
+        interleave(1, 1)
+        quantise(1, 0)
+        interleave(1, 2)
+        quantise(1, 1)
+        quantise(1, 2)
+        for e0, e1 in ((0, 2), (2, 4), (4, 8)):
+            gather(g_scales, scales, e0, e1)
+            gather(g_words[1], words[1], e0, e1)
 
-        for n, h in ((0, 0), (1, 0), (0, 1), (1, 1), (2, 0), (3, 0), (2, 1), (3, 1)):
-            relu = keep.tile([P, HALF], F32, name=f"relu{n}_{h}")
-            squared = keep.tile([P, HALF], F32, name=f"squared{n}_{h}")
-            for q in range(4):
-                e = 4 * h + q
-                place = slice(q * C, (q + 1) * C)
+        for n, e0, e1 in PIECES:
+            half = e0 // 4
+            width = (e1 - e0) * C
+            relu = keep.tile([P, width], F32, name=f"relu{n}_{e0}")
+            squared = keep.tile([P, width], F32, name=f"squared{n}_{e0}")
+            bank = banks[n][half]
+            for e in range(e0, e1):
+                place = slice((e - 4 * half) * C, (e - 4 * half + 1) * C)
                 slots = slice(e * C, (e + 1) * C)
                 w_cols = slice(e * N + n * P, e * N + (n + 1) * P)
                 nc.tensor.matmul_mx(
-                    out=banks[n][h][:, place],
+                    out=bank[:, place],
                     lhsT=w8_t[:, e, 4 * n * P : 4 * (n + 1) * P].bitcast(FP8X4),
                     lhsT_scale=w_sc[4:P, w_cols],
                     rhs=g_words[0][:, slots].bitcast(FP8X4),
@@ -137,7 +153,7 @@ def tile_moe_two_lin_relu2_kernel(tc, xT, w8_words, w8_scales, w4_words, w4_scal
                     stop=False,
                 )
                 nc.tensor.matmul_mx(
-                    out=banks[n][h][:, place],
+                    out=bank[:, place],
                     lhsT=w4_t[:, e, 2 * n * P : 2 * (n + 1) * P].bitcast(FP4X4),
                     lhsT_scale=w_sc[:, w_cols],
                     rhs=g_words[1][:, slots].bitcast(FP8X4),
@@ -145,13 +161,14 @@ def tile_moe_two_lin_relu2_kernel(tc, xT, w8_words, w8_scales, w4_words, w4_scal
                     start=False,
                     stop=True,
                 )
-                nc.scalar.activation(relu[:, place], banks[n][h][:, place], RELU, bias=bias[:, n, e : e + 1])
+            for e in range(e0, e1):
+                place = slice((e - 4 * half) * C, (e - 4 * half + 1) * C)
+                nc.scalar.activation(
+                    relu[:, (e - e0) * C : (e - e0 + 1) * C], bank[:, place], RELU, bias=bias[:, n, e : e + 1]
+                )
             nc.scalar.activation(squared[:], relu[:], SQUARE)
             nc.vector.tensor_tensor(
-                window[n][:].indirect(dst_t[:, 32 * h : 32 * h + 32]),
-                squared[:],
-                gate_t[:, h * HALF : (h + 1) * HALF],
-                MULT,
+                window[n][:].indirect(dst_t[:, 8 * e0 : 8 * e1]), squared[:], gate_t[:, e0 * C : e1 * C], MULT
             )
-            if h == 1:
+            if e1 == E:
                 nc.sync.dma_start(out=out[n * P : (n + 1) * P, :], in_=window[n][:])

import concourse.mybir as mybir

K, T, E, C, N = 1024, 1024, 8, 128, 512
P = 128
J = 4
FLOPS = 2 * K * N * E * C
BYTES = K * T * 4 + E * 128 * 512 * 6 + 2 * E * 16 * 512 + N * E * 4 + T * 4 + 2 * P * 64 * 2 + N * T * 4

F32 = mybir.dt.float32
BF16 = mybir.dt.bfloat16
U32 = mybir.dt.uint32
I32 = mybir.dt.int32
U16 = mybir.dt.uint16
U8 = mybir.dt.uint8
FP8X4 = mybir.dt.float8_e4m3fn_x4
FP4X4 = mybir.dt.float4_e2m1fn_x4
RELU = mybir.ActivationFunctionType.Relu
SQUARE = mybir.ActivationFunctionType.Square
MULT = mybir.AluOpType.mult

NT = N // P
HALF = T // 2
CHUNKS = (
    ((0, 512, 320), (512, 512, 320)),
    ((0, 512, 160), (512, 256, 128), (768, 256, 160)),
)
PLANE = (4, 0)
PIECES = (
    (0, 0, 2), (1, 0, 2), (0, 2, 4), (1, 2, 4), (0, 4, 8), (1, 4, 8),
    (2, 0, 4), (3, 0, 4), (2, 4, 8), (3, 4, 8),
)


def tile_moe_two_lin_relu2_kernel(tc, xT, w8_words, w8_scales, w4_words, w4_scales, b, gate, offs, dst, out):
    nc = tc.nc
    with tc.tile_pool(name="keep", bufs=1) as keep, tc.psum_pool(name="psum", bufs=1) as psum:
        offs_t = keep.tile([P, 64], U16, name="offs_t")
        dst_t = keep.tile([P, 64], U16, name="dst_t")
        bias = keep.tile([P, NT, E], F32, name="bias")
        gate_t = keep.tile([P, T], F32, name="gate_t")
        words = [keep.tile([P, T], U32, name=f"words{a}", align_bytes=256) for a in range(2)]
        scales = keep.tile([P, T], U8, name="scales", align_bytes=256)
        g_words = [keep.tile([P, T], U32, name=f"g_words{a}", align_bytes=256) for a in range(2)]
        g_scales = keep.tile([P, T], U8, name="g_scales", align_bytes=256)
        w8_t = keep.tile([P, E, 4 * N], U8, name="w8_t", align_bytes=256)
        w4_t = keep.tile([P, E, 2 * N], U8, name="w4_t", align_bytes=256)
        w_sc = keep.tile([P, E * N], U8, name="w_sc", align_bytes=256)
        window = [keep.tile([P, T], F32, name=f"window{n}") for n in range(NT)]
        banks = [[psum.tile([P, HALF], F32, name=f"bank{n}_{h}") for h in range(2)] for n in range(NT)]

        nc.gpsimd.memset(scales[:], 0)
        nc.vector.memset(w_sc[:].bitcast(I32), 0)

        def load_w8(e0, e1):
            nc.sync.dma_start(
                out=w8_t[:, e0:e1, :].bitcast(I32),
                in_=w8_words[e0:e1].rearrange("e a p n r -> (a p) e (n r)").bitcast(I32),
            )

        def load_w4(e0, e1):
            nc.sync.dma_start(
                out=w4_t[:, e0:e1, :].bitcast(I32), in_=w4_words[e0:e1].rearrange("e a p n -> (a p) e n").bitcast(I32)
            )

        def load_scales(r):
            for plane, sc in ((0, w4_scales), (4, w8_scales)):
                nc.sync.dma_start(
                    out=w_sc[plane + r : P : 32, :].bitcast(I32).rearrange("q (e n) -> q e n", e=E),
                    in_=sc.bitcast(I32).rearrange("e a (q r) n -> r a q e n", r=4)[r][0],
                )

        def load_gate(h):
            nc.sync.dma_start(out=gate_t[:, h * HALF : (h + 1) * HALF], in_=gate[0:P, h * HALF : (h + 1) * HALF])

        x_view = xT.rearrange("(a p j) t -> a p j t", a=2, j=J)
        raws, grouped = {}, {}
        for a in range(2):
            for i, (t0, width, v) in enumerate(CHUNKS[a]):
                raws[a, i] = keep.tile([P, J, width], F32, name=f"raw{a}_{i}")
                grouped[a, i] = keep.tile([P, width, J], BF16, name=f"grouped{a}_{i}", align_bytes=256)
                if (a, i) == (1, 2):
                    load_scales(0)
                    load_scales(1)
                nc.sync.dma_start(out=raws[a, i][:], in_=x_view[a][:, :, t0 : t0 + width])
                if (a, i) == (0, 0):
                    nc.sync.dma_start(offs_t[:], offs)

        load_w8(0, 2)
        load_scales(2)
        load_scales(3)
        nc.sync.dma_start(out=bias[:], in_=b.rearrange("(n p) e -> p n e", p=P))
        load_w4(0, 4)
        load_w8(2, 4)
        load_gate(0)
        nc.sync.dma_start(dst_t[:], dst)
        load_w8(4, 6)
        load_w4(4, 8)
        load_w8(6, 8)
        load_gate(1)

        def interleave(a, i):
            t0, width, v = CHUNKS[a][i]
            for copy, lo, hi in ((nc.vector.tensor_copy, 0, v), (nc.scalar.copy, v, width)):
                copy(
                    out=grouped[a, i][:, lo:hi, :].rearrange("p (c i) j -> p c j i", i=4),
                    in_=raws[a, i][:, :, lo:hi].rearrange("p j (c i) -> p c j i", i=4),
                )

        def quantise(a, i):
            t0, width, v = CHUNKS[a][i]
            nc.vector.quantize_mx(
                out=words[a][:, t0 : t0 + width].bitcast(FP8X4),
                scales=scales[PLANE[a] : P, t0 : t0 + width],
                in_=grouped[a, i][:].rearrange("p t j -> p (t j)"),
            )

        def gather(to, of, e0, e1):
            nc.vector.tensor_copy(to[:, e0 * C : e1 * C], of[:].indirect(offs_t[:, 8 * e0 : 8 * e1]))

        interleave(0, 0)
        interleave(0, 1)
        quantise(0, 0)
        quantise(0, 1)
        gather(g_words[0], words[0], 0, 4)
        gather(g_words[0], words[0], 4, 8)
        interleave(1, 0)
        interleave(1, 1)
        quantise(1, 0)
        interleave(1, 2)
        quantise(1, 1)
        quantise(1, 2)
        for e0, e1 in ((0, 2), (2, 4), (4, 8)):
            gather(g_scales, scales, e0, e1)
            gather(g_words[1], words[1], e0, e1)

        for n, e0, e1 in PIECES:
            half = e0 // 4
            width = (e1 - e0) * C
            relu = keep.tile([P, width], F32, name=f"relu{n}_{e0}")
            squared = keep.tile([P, width], F32, name=f"squared{n}_{e0}")
            bank = banks[n][half]
            for e in range(e0, e1):
                place = slice((e - 4 * half) * C, (e - 4 * half + 1) * C)
                slots = slice(e * C, (e + 1) * C)
                w_cols = slice(e * N + n * P, e * N + (n + 1) * P)
                nc.tensor.matmul_mx(
                    out=bank[:, place],
                    lhsT=w8_t[:, e, 4 * n * P : 4 * (n + 1) * P].bitcast(FP8X4),
                    lhsT_scale=w_sc[4:P, w_cols],
                    rhs=g_words[0][:, slots].bitcast(FP8X4),
                    rhs_scale=g_scales[4:P, slots],
                    start=True,
                    stop=False,
                )
                nc.tensor.matmul_mx(
                    out=bank[:, place],
                    lhsT=w4_t[:, e, 2 * n * P : 2 * (n + 1) * P].bitcast(FP4X4),
                    lhsT_scale=w_sc[:, w_cols],
                    rhs=g_words[1][:, slots].bitcast(FP8X4),
                    rhs_scale=g_scales[:, slots],
                    start=False,
                    stop=True,
                )
            for e in range(e0, e1):
                place = slice((e - 4 * half) * C, (e - 4 * half + 1) * C)
                nc.scalar.activation(
                    relu[:, (e - e0) * C : (e - e0 + 1) * C], bank[:, place], RELU, bias=bias[:, n, e : e + 1]
                )
            nc.scalar.activation(squared[:], relu[:], SQUARE)
            nc.vector.tensor_tensor(
                window[n][:].indirect(dst_t[:, 8 * e0 : 8 * e1]), squared[:], gate_t[:, e0 * C : e1 * C], MULT
            )
            if e1 == E:
                nc.sync.dma_start(out=out[n * P : (n + 1) * P, :], in_=window[n][:])
